import numpy as np
import ml_dtypes


def mxq(x, axis, fmt="e4m3"):
    dtype, down = {"e4m3": (ml_dtypes.float8_e4m3fn, 7), "e5m2": (ml_dtypes.float8_e5m2, 14)}[fmt]
    v = np.moveaxis(np.asarray(x, np.float32).astype(ml_dtypes.bfloat16).astype(np.float64), axis, -1)
    blocks = v.reshape(v.shape[:-1] + (-1, 32))
    amax = np.abs(blocks).max(-1, keepdims=True)
    byte = np.maximum(np.where(amax > 0, np.frexp(amax)[1] - 1 + 127, 0) - down, 1)
    scale = np.exp2(byte - 127.0)
    codes = (blocks / scale).astype(np.float32).astype(dtype).astype(np.float64)
    return np.moveaxis((codes * scale).reshape(v.shape), -1, axis)


WIDE = False


def mx_kscale(k):
    if not WIDE:
        return np.ones(k)
    levels = np.array([10, -10, 5, -5, 0])
    if k % 512:
        return np.exp2(np.random.permutation(np.resize(levels, k // 32))).repeat(32)
    a = np.empty((k // 512, 16))
    for p in range(k // 512):
        a[p, :8] = np.random.permutation(np.resize(levels, 8))
        for g in range(8):
            far = levels[np.abs(levels - a[p, g]) >= 10]
            a[p, g + 8] = far[np.random.randint(len(far))]
    return np.exp2(a.ravel()).repeat(32)


BF16 = ml_dtypes.bfloat16


def bf(x):
    return np.asarray(x, np.float32).astype(BF16)


def f64(x):
    return np.asarray(x).astype(np.float64)


E2M1 = np.array([0.0, 0.5, 1.0, 1.5, 2.0, 3.0, 4.0, 6.0, -0.0, -0.5, -1.0, -1.5, -2.0, -3.0, -4.0, -6.0])


def pack_weight(w, fmt):
    k, n = w.shape
    w = f64(bf(w)).reshape(k // 32, 32, n)
    amax = np.abs(w).max(1)
    if fmt == "e4m3":
        byte = np.frexp(amax)[1] - 1 + 127 - 7
    else:
        mant, ex = np.frexp(amax / 6.0)
        byte = np.where(mant > 0.5, ex, ex - 1) + 127
    byte = np.clip(np.where(amax > 0, byte, 1), 1, 254)
    scaled = (w * np.exp2(127.0 - byte)[:, None, :]).reshape(k, n).astype(np.float32)
    by_word = np.ascontiguousarray(scaled.reshape(k // 512, 128, 4, n).transpose(0, 1, 3, 2))
    if fmt == "e4m3":
        words = by_word.astype(ml_dtypes.float8_e4m3fn).view(np.uint8)
    else:
        c = by_word.astype(ml_dtypes.float4_e2m1fn).view(np.uint8) & 0xF
        words = c[..., 0::2] | (c[..., 1::2] << 4)
    return np.ascontiguousarray(words), np.ascontiguousarray(byte.astype(np.uint8).reshape(k // 512, 16, n))


def unpack_weight(words, scales, fmt):
    g, p, n, _ = words.shape
    if fmt == "e4m3":
        vals = np.ascontiguousarray(words).view(ml_dtypes.float8_e4m3fn).astype(np.float64)
    else:
        nib = np.empty((g, p, n, 4), np.uint8)
        nib[..., 0::2] = words & 0xF
        nib[..., 1::2] = words >> 4
        vals = E2M1[nib]
    vals = vals * np.repeat(np.exp2(scales.astype(np.float64) - 127.0), 8, axis=1)[..., None]
    return vals.transpose(0, 1, 3, 2).reshape(g * 512, n)
def pack4(w):
    words, scales = pack_weight(w, "e2m1")
    return words.reshape(words.shape[0], 128, -1), scales


def unpack4(words, scales):
    return unpack_weight(words.reshape(words.shape[0], 128, -1, 2), scales, "e2m1")


def planes(Y):
    n, m = Y.shape
    b = f64(bf(Y)).reshape(n // 32, 32, m)
    amax = np.abs(b).max(1)
    byte = np.clip(np.where(amax > 0, np.frexp(amax)[1] - 1 + 127 - 7, 1), 1, 254)
    codes = (b * np.exp2(127.0 - byte)[:, None, :]).reshape(n, m).astype(np.float32).astype(ml_dtypes.float8_e4m3fn).view(np.uint8)
    words = codes.reshape(n // 512, 128, 4, m).transpose(0, 1, 3, 2)
    return np.ascontiguousarray(words), np.ascontiguousarray(byte.astype(np.uint8).reshape(n // 512, 16, m))


T, R, F = 1536, 1024, 2048

def setup_inputs():
    s = mx_kscale(R)
    envelope = np.exp(0.5 * np.random.randn(F))
    H = np.abs(np.random.randn(T, R)) ** 3 / 1.6
    W = np.random.randn(R, F) ** 2 * envelope / R
    w_words, w_scales = pack4(W / s[:, None])
    background = 0.1 + 0.2 * np.abs(np.random.randn(F))
    V = envelope * np.exp(0.5 * np.random.randn(T, F))
    weight = np.exp(0.8 * np.random.randn(F))
    return {"h": bf(H * s), "w_words": w_words, "w_scales": w_scales,
            "background": bf(background), "v": bf(V), "weight": bf(weight)}

def reference(h, w_words, w_scales, background, v, weight):
    W = unpack4(w_words, w_scales)
    model = (mxq(f64(h), 1, "e4m3") @ W) + f64(background)
    y = f64(v) * (1.0 / model) * f64(weight)
    Y = y.T
    words, scales = planes(Y)
    return y, words, scales

@@ -1,0 +1,290 @@
+from contextlib import ExitStack
+
+import concourse.mybir as mybir
+from concourse.masks import make_identity
+
+T, R, F = 1536, 1024, 2048
+FLOPS = 2 * T * R * F
+
+F32 = mybir.dt.float32
+BF16 = mybir.dt.bfloat16
+I32 = mybir.dt.int32
+U32 = mybir.dt.uint32
+U8 = mybir.dt.uint8
+FP8X4 = mybir.dt.float8_e4m3fn_x4
+FP4X4 = mybir.dt.float4_e2m1fn_x4
+ACT = mybir.ActivationFunctionType
+ALU = mybir.AluOpType
+
+P = 128
+BANK = 512
+PASSES = R // 512
+ROWS = 4
+TBLOCKS = T // 512
+FGROUPS = F // 512
+GROUPS = TBLOCKS * FGROUPS
+STEPS = 2 * GROUPS
+STEPS_PER_BLOCK = 2 * FGROUPS
+
+
+def tile_weighted_kl_nmf_ratio_g4_kernel(
+    tc, h, w_words, w_scales, background, v, weight, out_0, out_1, out_2
+):
+    nc = tc.nc
+    with ExitStack() as ctx:
+        keep = ctx.enter_context(tc.tile_pool(name="keep", bufs=1))
+        work = ctx.enter_context(tc.tile_pool(name="work", bufs=2))
+        psum = ctx.enter_context(tc.psum_pool(name="psum", bufs=1))
+        ctx.enter_context(tc.manual_schedule())
+
+        ident = keep.tile([P, P], F32, name="ident")
+        bc_rows = keep.tile([P, P], BF16, name="bc_rows")
+        rows_rsqrt = keep.tile([P, P], F32, name="rows_rsqrt")
+        rows32 = keep.tile([P, 2, P], F32, name="rows32")
+        bc = keep.tile([P, 2 * P], F32, name="bc")
+        w_plane = keep.tile([P, PASSES, F], U8, name="w_plane", align_bytes=64)
+
+        h_raw, h_words, h_bank, h_turned, h_codes, h_plane = {}, {}, {}, {}, {}, {}
+        w_codes, v_raw = {}, {}
+        mx_bank, ratio, r_bank, y, y_words, y_bank, y_turned, y_codes, y_plane = (
+            {}, {}, {}, {}, {}, {}, {}, {}, {})
+
+        def bank(tag):
+            depth = {"mx": 2, "r": 3, "w": 2, "h": 1}[tag]
+            return psum.tile([P, BANK], F32, name="bank_" + tag, tag=tag, bufs=depth)
+
+        def load_h(tb, ps):
+            t = work.tile([P, ROWS, 512], BF16, name="h_raw", bufs=4)
+            src = h[512 * tb : 512 * (tb + 1), 512 * ps : 512 * (ps + 1)]
+            nc.sync.dma_start(out=t[:], in_=src.rearrange("(j p) k -> p j k", p=P))
+            h_raw[tb, ps] = t
+
+        def load_w(g):
+            t = work.tile([P, PASSES, 1024], U8, name="w_codes", bufs=FGROUPS, align_bytes=64)
+            src = w_words[:, :, 1024 * g : 1024 * (g + 1)].rearrange("s p b -> p s b")
+            nc.sync.dma_start(out=t[:].bitcast(I32), in_=src.bitcast(I32))
+            w_codes[g] = t
+
+        def load_v(grp):
+            tb, g = divmod(grp, FGROUPS)
+            t = work.tile([P, ROWS, 512], BF16, name="v_raw", bufs=4)
+            src = v[512 * tb : 512 * (tb + 1), 512 * g : 512 * (g + 1)]
+            nc.sync.dma_start(out=t[:], in_=src.rearrange("(j p) f -> p j f", p=P))
+            v_raw[grp] = t
+
+        def sort_h(tb, ps, jj):
+            if jj == 0:
+                h_words[tb, ps] = work.tile([P, ROWS, 2, P], F32, name="h_words", bufs=2)
+            src = h_raw[tb, ps][:].bitcast(F32)[:, 2 * jj : 2 * jj + 2, :]
+            nc.vector.tensor_copy(
+                out=h_words[tb, ps][:, 2 * jj : 2 * jj + 2],
+                in_=src.rearrange("p j (q u) -> p j u q", u=2))
+
+        def turn_h(tb, ps, jj, tag):
+            b = bank(tag)
+            for j2 in range(2):
+                for u in range(2):
+                    j = 2 * jj + j2
+                    if (tb, ps) in h_words:
+                        src = h_words[tb, ps][:, j, u, :]
+                    else:
+                        src = h_raw[tb, ps][:].bitcast(F32)[:, j, u::2]
+                    col = (2 * j2 + u) * P
+                    nc.tensor.transpose(b[:, col : col + P], src, ident[:])
+            h_bank[tb, ps, jj] = b
+
+        def interleave(eng, dst, jj, b):
+            out = dst[:].bitcast(F32)[:, 512 * jj : 512 * (jj + 1)].rearrange("p (j m u) -> p j m u", j=2, u=2)
+            src = b[:].rearrange("p (j u m) -> p j m u", j=2, u=2)
+            if eng == "scalar":
+                nc.scalar.copy(out=out, in_=src)
+            else:
+                nc.vector.tensor_copy(out=out, in_=src)
+
+        def drain_h(tb, ps, jj, eng):
+            if jj == 0:
+                h_turned[tb, ps] = work.tile([P, 2048], BF16, name="h_turned", bufs=2, align_bytes=64)
+            interleave(eng, h_turned[tb, ps], jj, h_bank[tb, ps, jj])
+
+        def quant_h(tb, ps):
+            codes = work.tile([P, 512], U32, name="h_codes", bufs=4, align_bytes=64)
+            plane = work.tile([P, 512], U8, name="h_plane", bufs=4, align_bytes=64)
+            nc.vector.quantize_mx(out=codes[:].bitcast(FP8X4), scales=plane[:], in_=h_turned[tb, ps][:])
+            h_codes[tb, ps], h_plane[tb, ps] = codes, plane
+
+        def multiply(k, order):
+            tb, g, half = k // STEPS_PER_BLOCK, (k // 2) % FGROUPS, k % 2
+            for b in range(2):
+                mx_bank[k, b] = bank("mx")
+            for b, ps in order:
+                col = 256 * half + P * b
+                nc.tensor.matmul_mx(
+                    out=mx_bank[k, b][:],
+                    lhsT=w_codes[g][:, ps, 2 * col : 2 * (col + P)].bitcast(FP4X4),
+                    lhsT_scale=w_plane[:, ps, 512 * g + col : 512 * g + col + P],
+                    rhs=h_codes[tb, ps][:].bitcast(FP8X4),
+                    rhs_scale=h_plane[tb, ps][:],
+                    start=(ps == 0),
+                    stop=(ps == PASSES - 1),
+                )
+
+        def invert(k):
+            fb0 = 2 * (k % STEPS_PER_BLOCK)
+            root = work.tile([P, 2, BANK], F32, name="root", bufs=2)
+            ratio[k] = work.tile([P, 2, BANK], F32, name="ratio", bufs=3)
+            for b in range(2):
+                nc.scalar.activation(out=root[:, b, :], in_=mx_bank[k, b][:], func=ACT.Abs_reciprocal_sqrt,
+                                     bias=bc[:, fb0 + b : fb0 + b + 1])
+            for b in range(2):
+                nc.scalar.activation(out=ratio[k][:, b, :], in_=root[:, b, :], func=ACT.Square,
+                                     scale=bc[:, P + 16 + fb0 + b : P + 16 + fb0 + b + 1])
+
+        def turn_ratio(k):
+            for jj in range(2):
+                bk = bank("r")
+                for j2 in range(2):
+                    for b in range(2):
+                        j = 2 * jj + j2
+                        col = (2 * j2 + b) * P
+                        nc.tensor.transpose(bk[:, col : col + P], ratio[k][:, b, P * j : P * (j + 1)], ident[:])
+                r_bank[k, jj] = bk
+
+        def apply_v(k, jj):
+            grp, half = divmod(k, 2)
+            if half == 0 and jj == 0:
+                y[grp] = work.tile([P, ROWS, 512], F32, name="y", bufs=3)
+            rows, cols = slice(2 * jj, 2 * jj + 2), slice(256 * half, 256 * (half + 1))
+            nc.vector.tensor_tensor(
+                out=y[grp][:, rows, cols],
+                in0=r_bank[k, jj][:].rearrange("p (j f) -> p j f", j=2),
+                in1=v_raw[grp][:, rows, cols],
+                op=ALU.mult)
+
+        def store_y(grp, rows):
+            tb, g = divmod(grp, FGROUPS)
+            dst = out_0[512 * tb : 512 * (tb + 1), 512 * g : 512 * (g + 1)].rearrange("(j p) f -> p j f", p=P)
+            nc.sync.dma_start(out=dst[:, rows, :], in_=y[grp][:, rows, :])
+
+        def round_y(unit):
+            grp, jj = divmod(unit, 2)
+            t = work.tile([P, 2, 2 * P, 2], BF16, name="y_words", bufs=3)
+            src = y[grp][:, 2 * jj : 2 * jj + 2, :].rearrange("p j (q u e) -> p u (j q) e", u=2, e=2)
+            nc.vector.tensor_copy(out=t[:], in_=src)
+            y_words[unit] = t
+
+        def turn_y(unit):
+            b = bank("w")
+            words = y_words[unit][:].rearrange("p u q e -> p (u q e)").bitcast(F32)
+            for j2 in range(2):
+                for u in range(2):
+                    src0 = (2 * u + j2) * P
+                    col = (2 * j2 + u) * P
+                    nc.tensor.transpose(b[:, col : col + P], words[:, src0 : src0 + P], ident[:])
+            y_bank[unit] = b
+
+        def drain_y(unit, eng):
+            grp, jj = divmod(unit, 2)
+            if jj == 0:
+                y_turned[grp] = work.tile([P, 2048], BF16, name="y_turned", bufs=2, align_bytes=64)
+            interleave(eng, y_turned[grp], jj, y_bank[unit])
+
+        def quant_y(grp):
+            tb, g = divmod(grp, FGROUPS)
+            if g == 0:
+                y_plane[tb] = work.tile([P, 512], U8, name="y_plane", bufs=2, align_bytes=64)
+            codes = work.tile([P, 512], U32, name="y_codes", bufs=3, align_bytes=64)
+            nc.vector.quantize_mx(out=codes[:].bitcast(FP8X4), scales=y_plane[tb][4 * g :, :], in_=y_turned[grp][:])
+            y_codes[grp] = codes
+
+        def store_planes(grp):
+            tb, g = divmod(grp, FGROUPS)
+            dst = out_1[g, :, 512 * tb : 512 * (tb + 1), :].rearrange("p m t -> p (m t)")
+            nc.sync.dma_start(out=dst.bitcast(I32), in_=y_codes[grp][:].bitcast(I32))
+            if g == FGROUPS - 1:
+                for q in range(4):
+                    dst = out_2[:, 4 * q : 4 * q + 4, 512 * tb : 512 * (tb + 1)]
+                    queue = nc.scalar if (grp == GROUPS - 1 and q % 2 == 1) else nc.sync
+                    queue.dma_start(out=dst.bitcast(I32), in_=y_plane[tb][32 * q : 32 * q + 16, :].bitcast(I32))
+
+        nc.vector.memset(bc_rows[:], 0.0)
+        nc.vector.memset(w_plane[:].bitcast(I32), 0)
+        make_identity(nc, ident[:])
+        nc.scalar.dma_start(out=bc_rows[0:16, :], in_=background.rearrange("(c p) -> c p", p=P))
+        nc.scalar.dma_start(out=bc_rows[16:32, :], in_=weight.rearrange("(c p) -> c p", p=P))
+        load_h(0, 0)
+        load_h(0, 1)
+        for q in range(4):
+            src = w_scales[:, 4 * q : 4 * q + 4, :].rearrange("s r n -> r s n")
+            nc.scalar.dma_start(out=w_plane[32 * q : 32 * q + 4].bitcast(I32), in_=src.bitcast(I32))
+        load_w(0)
+        load_v(0)
+        load_w(1)
+        load_v(1)
+        load_w(2)
+        load_w(3)
+
+        nc.scalar.activation(out=rows_rsqrt[:], in_=bc_rows[:], func=ACT.Abs_reciprocal_sqrt, bias=2.0 ** -86)
+        sort_h(0, 0, 0)
+        sort_h(0, 0, 1)
+        turn_h(0, 0, 0, "w")
+        turn_h(0, 0, 1, "w")
+        sort_h(0, 1, 0)
+        sort_h(0, 1, 1)
+        turn_h(0, 1, 0, "r")
+        turn_h(0, 1, 1, "r")
+        nc.vector.tensor_copy(out=rows32[:, 0, :], in_=bc_rows[:])
+        nc.vector.tensor_tensor(out=rows32[:, 1, :], in0=bc_rows[:], in1=rows_rsqrt[:], op=ALU.mult)
+        bc_bank = bank("h")
+        for i in range(2):
+            nc.tensor.transpose(bc_bank[:, P * i : P * (i + 1)], rows32[:, i, :], ident[:])
+        drain_h(0, 0, 0, "scalar")
+        drain_h(0, 0, 1, "vector")
+        drain_h(0, 1, 0, "scalar")
+        quant_h(0, 0)
+        drain_h(0, 1, 1, "scalar")
+        nc.vector.tensor_copy(out=bc[:], in_=bc_bank[:, 0 : 2 * P])
+        quant_h(0, 1)
+
+        H_TURN_AT = {0: (0, 0), 2: (0, 1), 4: (1, 0), 5: (1, 1)}
+        H_QUANT_AT = {5: 0, 7: 1}
+        for k in range(STEPS + 6):
+            tb, i = divmod(k, STEPS_PER_BLOCK)
+            nxt = tb + 1 if tb + 1 < TBLOCKS else None
+            if k % 2 == 0 and k // 2 + 2 < GROUPS:
+                load_v(k // 2 + 2)
+            if k == 0:
+                load_h(1, 0)
+                load_h(1, 1)
+            if k == 5:
+                load_h(2, 0)
+                load_h(2, 1)
+            y_drain_eng = "scalar" if (k >= 2 * STEPS_PER_BLOCK and k % 2 == 1) or k >= STEPS else "vector"
+            if nxt is not None and i - 1 in H_TURN_AT:
+                drain_h(nxt, *H_TURN_AT[i - 1], "scalar")
+            if 0 <= k - 4 < STEPS and y_drain_eng == "scalar":
+                drain_y(k - 4, "scalar")
+            if k < STEPS:
+                multiply(k, [(0, 0), (1, 0), (0, 1), (1, 1)] if k == 0 else [(0, 0), (0, 1), (1, 0), (1, 1)])
+                invert(k)
+            if 0 <= k - 3 < STEPS:
+                round_y(k - 3)
+            if 0 <= k - 4 < STEPS and y_drain_eng == "vector":
+                drain_y(k - 4, "vector")
+            if k >= 6 and k % 2 == 0:
+                quant_y((k - 6) // 2)
+                store_planes((k - 6) // 2)
+            if nxt is not None and i in H_QUANT_AT:
+                quant_h(nxt, H_QUANT_AT[i])
+            if 0 <= k - 1 < STEPS:
+                turn_ratio(k - 1)
+            if 0 <= k - 3 < STEPS:
+                turn_y(k - 3)
+            if nxt is not None and i in H_TURN_AT:
+                turn_h(nxt, *H_TURN_AT[i], "h")
+            if 0 <= k - 1 < STEPS:
+                for jj in range(2):
+                    apply_v(k - 1, jj)
+                    if k == STEPS:
+                        store_y(GROUPS - 1, slice(2 * jj, 2 * jj + 2))
+                if k % 2 == 0 and k < STEPS:
+                    store_y((k - 1) // 2, slice(0, ROWS))

@@ -53,11 +53,12 @@ def tile_weighted_kl_nmf_ratio_g4_kernel(
             depth = {"mx": 2, "r": 3, "w": 2, "h": 1}[tag]
             return psum.tile([P, BANK], F32, name="bank_" + tag, tag=tag, bufs=depth)
 
-        def load_h(tb, ps):
-            t = work.tile([P, ROWS, 512], BF16, name="h_raw", bufs=4)
-            src = h[512 * tb : 512 * (tb + 1), 512 * ps : 512 * (ps + 1)]
+        def load_h(tb, ps, jj):
+            t = work.tile([P, 2, 512], BF16, name="h_raw", bufs=8)
+            r0 = 512 * tb + 256 * jj
+            src = h[r0 : r0 + 256, 512 * ps : 512 * (ps + 1)]
             nc.sync.dma_start(out=t[:], in_=src.rearrange("(j p) k -> p j k", p=P))
-            h_raw[tb, ps] = t
+            h_raw[tb, ps, jj] = t
 
         def load_w(g):
             t = work.tile([P, PASSES, 1024], U8, name="w_codes", bufs=FGROUPS, align_bytes=64)
@@ -73,22 +74,19 @@ def tile_weighted_kl_nmf_ratio_g4_kernel(
             v_raw[grp] = t
 
         def sort_h(tb, ps, jj):
-            if jj == 0:
-                h_words[tb, ps] = work.tile([P, ROWS, 2, P], F32, name="h_words", bufs=2)
-            src = h_raw[tb, ps][:].bitcast(F32)[:, 2 * jj : 2 * jj + 2, :]
-            nc.vector.tensor_copy(
-                out=h_words[tb, ps][:, 2 * jj : 2 * jj + 2],
-                in_=src.rearrange("p j (q u) -> p j u q", u=2))
+            t = work.tile([P, 2, 2, P], F32, name="h_words", bufs=4)
+            src = h_raw[tb, ps, jj][:].bitcast(F32)
+            nc.vector.tensor_copy(out=t[:], in_=src.rearrange("p j (q u) -> p j u q", u=2))
+            h_words[tb, ps, jj] = t
 
         def turn_h(tb, ps, jj, tag):
             b = bank(tag)
             for j2 in range(2):
                 for u in range(2):
-                    j = 2 * jj + j2
-                    if (tb, ps) in h_words:
-                        src = h_words[tb, ps][:, j, u, :]
+                    if (tb, ps, jj) in h_words:
+                        src = h_words[tb, ps, jj][:, j2, u, :]
                     else:
-                        src = h_raw[tb, ps][:].bitcast(F32)[:, j, u::2]
+                        src = h_raw[tb, ps, jj][:].bitcast(F32)[:, j2, u::2]
                     col = (2 * j2 + u) * P
                     nc.tensor.transpose(b[:, col : col + P], src, ident[:])
             h_bank[tb, ps, jj] = b
@@ -169,7 +167,10 @@ def tile_weighted_kl_nmf_ratio_g4_kernel(
             grp, jj = divmod(unit, 2)
             t = work.tile([P, 2, 2 * P, 2], BF16, name="y_words", bufs=3)
             src = y[grp][:, 2 * jj : 2 * jj + 2, :].rearrange("p j (q u e) -> p u (j q) e", u=2, e=2)
-            nc.vector.tensor_copy(out=t[:], in_=src)
+            if unit < STEPS - 2:
+                nc.gpsimd.tensor_scalar(out=t[:], in0=src, scalar1=1.0, scalar2=0.0, op0=ALU.mult, op1=ALU.add)
+            else:
+                nc.vector.tensor_copy(out=t[:], in_=src)
             y_words[unit] = t
 
         def turn_y(unit):
@@ -188,19 +189,17 @@ def tile_weighted_kl_nmf_ratio_g4_kernel(
                 y_turned[grp] = work.tile([P, 2048], BF16, name="y_turned", bufs=2, align_bytes=64)
             interleave(eng, y_turned[grp], jj, y_bank[unit])
 
-        def quant_y(grp):
+        def quant_y(grp, m0, m1):
             tb, g = divmod(grp, FGROUPS)
-            if g == 0:
-                y_plane[tb] = work.tile([P, 512], U8, name="y_plane", bufs=2, align_bytes=64)
-            codes = work.tile([P, 512], U32, name="y_codes", bufs=3, align_bytes=64)
-            nc.vector.quantize_mx(out=codes[:].bitcast(FP8X4), scales=y_plane[tb][4 * g :, :], in_=y_turned[grp][:])
-            y_codes[grp] = codes
-
-        def store_planes(grp):
-            tb, g = divmod(grp, FGROUPS)
-            dst = out_1[g, :, 512 * tb : 512 * (tb + 1), :].rearrange("p m t -> p (m t)")
-            nc.sync.dma_start(out=dst.bitcast(I32), in_=y_codes[grp][:].bitcast(I32))
-            if g == FGROUPS - 1:
+            if m0 == 0:
+                if g == 0:
+                    y_plane[tb] = work.tile([P, 512], U8, name="y_plane", bufs=2, align_bytes=64)
+                y_codes[grp] = work.tile([P, 512], U32, name="y_codes", bufs=3, align_bytes=64)
+            nc.vector.quantize_mx(out=y_codes[grp][:, m0:m1].bitcast(FP8X4), scales=y_plane[tb][4 * g :, m0:m1],
+                                  in_=y_turned[grp][:, 4 * m0 : 4 * m1])
+            dst = out_1[g, :, 512 * tb + m0 : 512 * tb + m1, :].rearrange("p m t -> p (m t)")
+            nc.sync.dma_start(out=dst.bitcast(I32), in_=y_codes[grp][:, m0:m1].bitcast(I32))
+            if g == FGROUPS - 1 and m1 == 512:
                 for q in range(4):
                     dst = out_2[:, 4 * q : 4 * q + 4, 512 * tb : 512 * (tb + 1)]
                     queue = nc.scalar if (grp == GROUPS - 1 and q % 2 == 1) else nc.sync
@@ -211,17 +210,22 @@ def tile_weighted_kl_nmf_ratio_g4_kernel(
         make_identity(nc, ident[:])
         nc.scalar.dma_start(out=bc_rows[0:16, :], in_=background.rearrange("(c p) -> c p", p=P))
         nc.scalar.dma_start(out=bc_rows[16:32, :], in_=weight.rearrange("(c p) -> c p", p=P))
-        load_h(0, 0)
-        load_h(0, 1)
+        for ps in range(PASSES):
+            for jj in range(2):
+                load_h(0, ps, jj)
         for q in range(4):
             src = w_scales[:, 4 * q : 4 * q + 4, :].rearrange("s r n -> r s n")
-            nc.scalar.dma_start(out=w_plane[32 * q : 32 * q + 4].bitcast(I32), in_=src.bitcast(I32))
+            nc.sync.dma_start(out=w_plane[32 * q : 32 * q + 4].bitcast(I32), in_=src.bitcast(I32))
         load_w(0)
         load_v(0)
         load_w(1)
+        load_h(1, 0, 0)
         load_v(1)
+        load_h(1, 0, 1)
         load_w(2)
         load_w(3)
+        load_h(1, 1, 0)
+        load_h(1, 1, 1)
 
         nc.scalar.activation(out=rows_rsqrt[:], in_=bc_rows[:], func=ACT.Abs_reciprocal_sqrt, bias=2.0 ** -86)
         sort_h(0, 0, 0)
@@ -245,22 +249,20 @@ def tile_weighted_kl_nmf_ratio_g4_kernel(
         nc.vector.tensor_copy(out=bc[:], in_=bc_bank[:, 0 : 2 * P])
         quant_h(0, 1)
 
-        H_TURN_AT = {0: (0, 0), 2: (0, 1), 4: (1, 0), 5: (1, 1)}
-        H_QUANT_AT = {5: 0, 7: 1}
-        for k in range(STEPS + 6):
+        H_TURN_AT = {1: (0, 0), 2: (0, 1), 4: (1, 0), 5: (1, 1)}
+        H_QUANT_AT = {4: 0, 6: 1}
+        for k in range(STEPS + 5):
             tb, i = divmod(k, STEPS_PER_BLOCK)
             nxt = tb + 1 if tb + 1 < TBLOCKS else None
             if k % 2 == 0 and k // 2 + 2 < GROUPS:
                 load_v(k // 2 + 2)
-            if k == 0:
-                load_h(1, 0)
-                load_h(1, 1)
-            if k == 5:
-                load_h(2, 0)
-                load_h(2, 1)
-            y_drain_eng = "scalar" if (k >= 2 * STEPS_PER_BLOCK and k % 2 == 1) or k >= STEPS else "vector"
-            if nxt is not None and i - 1 in H_TURN_AT:
-                drain_h(nxt, *H_TURN_AT[i - 1], "scalar")
+            if k in (3, 5):
+                load_h(2, (k - 3) // 2, 0)
+                load_h(2, (k - 3) // 2, 1)
+            h_drain = H_TURN_AT[i - 1] if nxt is not None and i - 1 in H_TURN_AT else None
+            y_drain_eng = "scalar" if k - 4 >= STEPS - 4 else "vector"
+            if h_drain is not None and h_drain[1] == 1:
+                drain_h(nxt, *h_drain, "scalar")
             if 0 <= k - 4 < STEPS and y_drain_eng == "scalar":
                 drain_y(k - 4, "scalar")
             if k < STEPS:
@@ -270,9 +272,12 @@ def tile_weighted_kl_nmf_ratio_g4_kernel(
                 round_y(k - 3)
             if 0 <= k - 4 < STEPS and y_drain_eng == "vector":
                 drain_y(k - 4, "vector")
-            if k >= 6 and k % 2 == 0:
-                quant_y((k - 6) // 2)
-                store_planes((k - 6) // 2)
+            if h_drain is not None and h_drain[1] == 0:
+                drain_h(nxt, *h_drain, "vector")
+            if 6 <= k < STEPS + 4 and k % 2 == 0:
+                quant_y((k - 6) // 2, 0, 512)
+            if k >= STEPS + 3:
+                quant_y(GROUPS - 1, 256 * (k - STEPS - 3), 256 * (k - STEPS - 2))
             if nxt is not None and i in H_QUANT_AT:
                 quant_h(nxt, H_QUANT_AT[i])
             if 0 <= k - 1 < STEPS:

@@ -50,7 +50,7 @@ def tile_weighted_kl_nmf_ratio_g4_kernel(
             {}, {}, {}, {}, {}, {}, {}, {}, {})
 
         def bank(tag):
-            depth = {"mx": 2, "r": 3, "w": 2, "h": 1}[tag]
+            depth = {"mx": 2, "r": 3, "w": 1, "h": 2}[tag]
             return psum.tile([P, BANK], F32, name="bank_" + tag, tag=tag, bufs=depth)
 
         def load_h(tb, ps, jj):
@@ -79,9 +79,11 @@ def tile_weighted_kl_nmf_ratio_g4_kernel(
             nc.vector.tensor_copy(out=t[:], in_=src.rearrange("p j (q u) -> p j u q", u=2))
             h_words[tb, ps, jj] = t
 
-        def turn_h(tb, ps, jj, tag):
-            b = bank(tag)
-            for j2 in range(2):
+        def turn_h(tb, ps, jj, tag, rows=(0, 1)):
+            if rows[0] == 0:
+                h_bank[tb, ps, jj] = bank(tag)
+            b = h_bank[tb, ps, jj]
+            for j2 in rows:
                 for u in range(2):
                     if (tb, ps, jj) in h_words:
                         src = h_words[tb, ps, jj][:, j2, u, :]
@@ -89,7 +91,6 @@ def tile_weighted_kl_nmf_ratio_g4_kernel(
                         src = h_raw[tb, ps, jj][:].bitcast(F32)[:, j2, u::2]
                     col = (2 * j2 + u) * P
                     nc.tensor.transpose(b[:, col : col + P], src, ident[:])
-            h_bank[tb, ps, jj] = b
 
         def interleave(eng, dst, jj, b):
             out = dst[:].bitcast(F32)[:, 512 * jj : 512 * (jj + 1)].rearrange("p (j m u) -> p j m u", j=2, u=2)
@@ -104,11 +105,12 @@ def tile_weighted_kl_nmf_ratio_g4_kernel(
                 h_turned[tb, ps] = work.tile([P, 2048], BF16, name="h_turned", bufs=2, align_bytes=64)
             interleave(eng, h_turned[tb, ps], jj, h_bank[tb, ps, jj])
 
-        def quant_h(tb, ps):
-            codes = work.tile([P, 512], U32, name="h_codes", bufs=4, align_bytes=64)
-            plane = work.tile([P, 512], U8, name="h_plane", bufs=4, align_bytes=64)
-            nc.vector.quantize_mx(out=codes[:].bitcast(FP8X4), scales=plane[:], in_=h_turned[tb, ps][:])
-            h_codes[tb, ps], h_plane[tb, ps] = codes, plane
+        def quant_h(tb, ps, m0=0, m1=512):
+            if m0 == 0:
+                h_codes[tb, ps] = work.tile([P, 512], U32, name="h_codes", bufs=4, align_bytes=64)
+                h_plane[tb, ps] = work.tile([P, 512], U8, name="h_plane", bufs=4, align_bytes=64)
+            nc.vector.quantize_mx(out=h_codes[tb, ps][:, m0:m1].bitcast(FP8X4), scales=h_plane[tb, ps][:, m0:m1],
+                                  in_=h_turned[tb, ps][:, 4 * m0 : 4 * m1])
 
         def multiply(k, order):
             tb, g, half = k // STEPS_PER_BLOCK, (k // 2) % FGROUPS, k % 2
@@ -174,7 +176,7 @@ def tile_weighted_kl_nmf_ratio_g4_kernel(
             y_words[unit] = t
 
         def turn_y(unit):
-            b = bank("w")
+            b = bank("h" if unit >= STEPS - 4 and unit % 2 == 1 else "w")
             words = y_words[unit][:].rearrange("p u q e -> p (u q e)").bitcast(F32)
             for j2 in range(2):
                 for u in range(2):
@@ -217,76 +219,73 @@ def tile_weighted_kl_nmf_ratio_g4_kernel(
             src = w_scales[:, 4 * q : 4 * q + 4, :].rearrange("s r n -> r s n")
             nc.sync.dma_start(out=w_plane[32 * q : 32 * q + 4].bitcast(I32), in_=src.bitcast(I32))
         load_w(0)
-        load_v(0)
-        load_w(1)
         load_h(1, 0, 0)
-        load_v(1)
+        load_v(0)
         load_h(1, 0, 1)
+        load_w(1)
+        load_h(1, 1, 0)
+        load_v(1)
+        load_h(1, 1, 1)
         load_w(2)
         load_w(3)
-        load_h(1, 1, 0)
-        load_h(1, 1, 1)
 
         nc.scalar.activation(out=rows_rsqrt[:], in_=bc_rows[:], func=ACT.Abs_reciprocal_sqrt, bias=2.0 ** -86)
         sort_h(0, 0, 0)
         sort_h(0, 0, 1)
-        turn_h(0, 0, 0, "w")
-        turn_h(0, 0, 1, "w")
+        turn_h(0, 0, 0, "h")
+        turn_h(0, 0, 1, "h")
         sort_h(0, 1, 0)
         sort_h(0, 1, 1)
         turn_h(0, 1, 0, "r")
         turn_h(0, 1, 1, "r")
-        nc.vector.tensor_copy(out=rows32[:, 0, :], in_=bc_rows[:])
-        nc.vector.tensor_tensor(out=rows32[:, 1, :], in0=bc_rows[:], in1=rows_rsqrt[:], op=ALU.mult)
-        bc_bank = bank("h")
-        for i in range(2):
-            nc.tensor.transpose(bc_bank[:, P * i : P * (i + 1)], rows32[:, i, :], ident[:])
         drain_h(0, 0, 0, "scalar")
         drain_h(0, 0, 1, "vector")
+        nc.vector.tensor_copy(out=rows32[:, 0, :], in_=bc_rows[:])
+        nc.vector.tensor_tensor(out=rows32[:, 1, :], in0=bc_rows[:], in1=rows_rsqrt[:], op=ALU.mult)
+        bc_bank = bank("w")
+        for i in range(2):
+            nc.tensor.transpose(bc_bank[:, P * i : P * (i + 1)], rows32[:, i, :], ident[:])
         drain_h(0, 1, 0, "scalar")
         quant_h(0, 0)
         drain_h(0, 1, 1, "scalar")
-        nc.vector.tensor_copy(out=bc[:], in_=bc_bank[:, 0 : 2 * P])
-        quant_h(0, 1)
+        nc.scalar.copy(out=bc[:], in_=bc_bank[:, 0 : 2 * P])
+        quant_h(0, 1, 0, 256)
+        quant_h(0, 1, 256, 512)
 
-        H_TURN_AT = {1: (0, 0), 2: (0, 1), 4: (1, 0), 5: (1, 1)}
-        H_QUANT_AT = {4: 0, 6: 1}
+        h_turns, h_drains, h_quants = {}, {}, {4: (1, 0), 6: (1, 1), 10: (2, 0), 14: (2, 1)}
+        for c in range(4):
+            ps, jj = divmod(c, 2)
+            h_turns[c] = (1, ps, jj, "h", (0, 1))
+            h_drains[c + 1] = (1, ps, jj)
+            h_turns[5 + 2 * c] = (2, ps, jj, "h", (0,))
+            h_turns[6 + 2 * c] = (2, ps, jj, "h", (1,))
+            h_drains[7 + 2 * c] = (2, ps, jj)
         for k in range(STEPS + 5):
-            tb, i = divmod(k, STEPS_PER_BLOCK)
-            nxt = tb + 1 if tb + 1 < TBLOCKS else None
             if k % 2 == 0 and k // 2 + 2 < GROUPS:
                 load_v(k // 2 + 2)
-            if k in (3, 5):
-                load_h(2, (k - 3) // 2, 0)
-                load_h(2, (k - 3) // 2, 1)
-            h_drain = H_TURN_AT[i - 1] if nxt is not None and i - 1 in H_TURN_AT else None
-            y_drain_eng = "scalar" if k - 4 >= STEPS - 4 else "vector"
-            if h_drain is not None and h_drain[1] == 1:
-                drain_h(nxt, *h_drain, "scalar")
-            if 0 <= k - 4 < STEPS and y_drain_eng == "scalar":
-                drain_y(k - 4, "scalar")
+            if k in (1, 3):
+                load_h(2, (k - 1) // 2, 0)
+                load_h(2, (k - 1) // 2, 1)
             if k < STEPS:
                 multiply(k, [(0, 0), (1, 0), (0, 1), (1, 1)] if k == 0 else [(0, 0), (0, 1), (1, 0), (1, 1)])
                 invert(k)
             if 0 <= k - 3 < STEPS:
                 round_y(k - 3)
-            if 0 <= k - 4 < STEPS and y_drain_eng == "vector":
-                drain_y(k - 4, "vector")
-            if h_drain is not None and h_drain[1] == 0:
-                drain_h(nxt, *h_drain, "vector")
+            if k in h_drains:
+                drain_h(*h_drains[k], "vector")
             if 6 <= k < STEPS + 4 and k % 2 == 0:
                 quant_y((k - 6) // 2, 0, 512)
+            if k in h_quants:
+                quant_h(*h_quants[k])
+            if 0 <= k - 4 < STEPS:
+                turn_y(k - 4)
+                drain_y(k - 4, "scalar" if k >= STEPS else "vector")
             if k >= STEPS + 3:
                 quant_y(GROUPS - 1, 256 * (k - STEPS - 3), 256 * (k - STEPS - 2))
-            if nxt is not None and i in H_QUANT_AT:
-                quant_h(nxt, H_QUANT_AT[i])
+            if k in h_turns:
+                turn_h(*h_turns[k])
             if 0 <= k - 1 < STEPS:
                 turn_ratio(k - 1)
-            if 0 <= k - 3 < STEPS:
-                turn_y(k - 3)
-            if nxt is not None and i in H_TURN_AT:
-                turn_h(nxt, *H_TURN_AT[i], "h")
-            if 0 <= k - 1 < STEPS:
                 for jj in range(2):
                     apply_v(k - 1, jj)
                     if k == STEPS:

@@ -53,29 +53,32 @@ def tile_weighted_kl_nmf_ratio_g4_kernel(
             depth = {"mx": 2, "r": 3, "w": 1, "h": 2}[tag]
             return psum.tile([P, BANK], F32, name="bank_" + tag, tag=tag, bufs=depth)
 
-        def load_h(tb, ps, jj):
-            t = work.tile([P, 2, 512], BF16, name="h_raw", bufs=8)
-            r0 = 512 * tb + 256 * jj
-            src = h[r0 : r0 + 256, 512 * ps : 512 * (ps + 1)]
+        def load_h(tb, jj, passes):
+            width = 512 * len(passes)
+            t = work.tile([P, 2, width], BF16, name="h_raw%d" % width, bufs=4)
+            r0, c0 = 512 * tb + 256 * jj, 512 * passes[0]
+            src = h[r0 : r0 + 256, c0 : c0 + width]
             nc.sync.dma_start(out=t[:], in_=src.rearrange("(j p) k -> p j k", p=P))
-            h_raw[tb, ps, jj] = t
+            for n, ps in enumerate(passes):
+                h_raw[tb, ps, jj] = t[:].bitcast(F32)[:, :, 256 * n : 256 * (n + 1)]
 
-        def load_w(g):
-            t = work.tile([P, PASSES, 1024], U8, name="w_codes", bufs=FGROUPS, align_bytes=64)
-            src = w_words[:, :, 1024 * g : 1024 * (g + 1)].rearrange("s p b -> p s b")
+        def load_w(g0, g1):
+            t = keep.tile([P, PASSES, 1024 * (g1 - g0)], U8, name="w_codes%d" % g0, align_bytes=64)
+            src = w_words[:, :, 1024 * g0 : 1024 * g1].rearrange("s p b -> p s b")
             nc.sync.dma_start(out=t[:].bitcast(I32), in_=src.bitcast(I32))
-            w_codes[g] = t
+            for g in range(g0, g1):
+                w_codes[g] = t[:, :, 1024 * (g - g0) : 1024 * (g - g0 + 1)]
 
-        def load_v(grp):
-            tb, g = divmod(grp, FGROUPS)
-            t = work.tile([P, ROWS, 512], BF16, name="v_raw", bufs=4)
-            src = v[512 * tb : 512 * (tb + 1), 512 * g : 512 * (g + 1)]
+        def load_v(tb, g0, g1):
+            t = keep.tile([P, ROWS, 512 * (g1 - g0)], BF16, name="v_raw%d_%d" % (tb, g0))
+            src = v[512 * tb : 512 * (tb + 1), 512 * g0 : 512 * g1]
             nc.sync.dma_start(out=t[:], in_=src.rearrange("(j p) f -> p j f", p=P))
-            v_raw[grp] = t
+            for g in range(g0, g1):
+                v_raw[FGROUPS * tb + g] = t[:, :, 512 * (g - g0) : 512 * (g - g0 + 1)]
 
         def sort_h(tb, ps, jj):
             t = work.tile([P, 2, 2, P], F32, name="h_words", bufs=4)
-            src = h_raw[tb, ps, jj][:].bitcast(F32)
+            src = h_raw[tb, ps, jj]
             nc.vector.tensor_copy(out=t[:], in_=src.rearrange("p j (q u) -> p j u q", u=2))
             h_words[tb, ps, jj] = t
 
@@ -88,7 +91,7 @@ def tile_weighted_kl_nmf_ratio_g4_kernel(
                     if (tb, ps, jj) in h_words:
                         src = h_words[tb, ps, jj][:, j2, u, :]
                     else:
-                        src = h_raw[tb, ps, jj][:].bitcast(F32)[:, j2, u::2]
+                        src = h_raw[tb, ps, jj][:, j2, u::2]
                     col = (2 * j2 + u) * P
                     nc.tensor.transpose(b[:, col : col + P], src, ident[:])
 
@@ -152,7 +155,7 @@ def tile_weighted_kl_nmf_ratio_g4_kernel(
         def apply_v(k, jj):
             grp, half = divmod(k, 2)
             if half == 0 and jj == 0:
-                y[grp] = work.tile([P, ROWS, 512], F32, name="y", bufs=3)
+                y[grp] = work.tile([P, ROWS, 512], F32, name="y", bufs=4)
             rows, cols = slice(2 * jj, 2 * jj + 2), slice(256 * half, 256 * (half + 1))
             nc.vector.tensor_tensor(
                 out=y[grp][:, rows, cols],
@@ -160,10 +163,10 @@ def tile_weighted_kl_nmf_ratio_g4_kernel(
                 in1=v_raw[grp][:, rows, cols],
                 op=ALU.mult)
 
-        def store_y(grp, rows):
+        def store_y(grp, rows, cols):
             tb, g = divmod(grp, FGROUPS)
             dst = out_0[512 * tb : 512 * (tb + 1), 512 * g : 512 * (g + 1)].rearrange("(j p) f -> p j f", p=P)
-            nc.sync.dma_start(out=dst[:, rows, :], in_=y[grp][:, rows, :])
+            nc.sync.dma_start(out=dst[:, rows, cols], in_=y[grp][:, rows, cols])
 
         def round_y(unit):
             grp, jj = divmod(unit, 2)
@@ -214,20 +217,19 @@ def tile_weighted_kl_nmf_ratio_g4_kernel(
         nc.scalar.dma_start(out=bc_rows[16:32, :], in_=weight.rearrange("(c p) -> c p", p=P))
         for ps in range(PASSES):
             for jj in range(2):
-                load_h(0, ps, jj)
+                load_h(0, jj, (ps,))
         for q in range(4):
             src = w_scales[:, 4 * q : 4 * q + 4, :].rearrange("s r n -> r s n")
             nc.sync.dma_start(out=w_plane[32 * q : 32 * q + 4].bitcast(I32), in_=src.bitcast(I32))
-        load_w(0)
-        load_h(1, 0, 0)
-        load_v(0)
-        load_h(1, 0, 1)
-        load_w(1)
-        load_h(1, 1, 0)
-        load_v(1)
-        load_h(1, 1, 1)
-        load_w(2)
-        load_w(3)
+        load_w(0, 1)
+        load_h(1, 0, (0, 1))
+        load_v(0, 0, 1)
+        load_h(1, 1, (0, 1))
+        load_w(1, FGROUPS)
+        load_v(0, 1, FGROUPS)
+        load_h(2, 0, (0, 1))
+        load_h(2, 1, (0, 1))
+        load_v(1, 0, FGROUPS)
 
         nc.scalar.activation(out=rows_rsqrt[:], in_=bc_rows[:], func=ACT.Abs_reciprocal_sqrt, bias=2.0 ** -86)
         sort_h(0, 0, 0)
@@ -261,11 +263,8 @@ def tile_weighted_kl_nmf_ratio_g4_kernel(
             h_turns[6 + 2 * c] = (2, ps, jj, "h", (1,))
             h_drains[7 + 2 * c] = (2, ps, jj)
         for k in range(STEPS + 5):
-            if k % 2 == 0 and k // 2 + 2 < GROUPS:
-                load_v(k // 2 + 2)
-            if k in (1, 3):
-                load_h(2, (k - 1) // 2, 0)
-                load_h(2, (k - 1) // 2, 1)
+            if k == 6:
+                load_v(2, 0, FGROUPS)
             if k < STEPS:
                 multiply(k, [(0, 0), (1, 0), (0, 1), (1, 1)] if k == 0 else [(0, 0), (0, 1), (1, 0), (1, 1)])
                 invert(k)
@@ -289,6 +288,8 @@ def tile_weighted_kl_nmf_ratio_g4_kernel(
                 for jj in range(2):
                     apply_v(k - 1, jj)
                     if k == STEPS:
-                        store_y(GROUPS - 1, slice(2 * jj, 2 * jj + 2))
+                        store_y(GROUPS - 1, slice(2 * jj, 2 * jj + 2), slice(256, 512))
                 if k % 2 == 0 and k < STEPS:
-                    store_y((k - 1) // 2, slice(0, ROWS))
+                    store_y((k - 1) // 2, slice(0, ROWS), slice(0, 512))
+                if k == STEPS - 1:
+                    store_y(GROUPS - 1, slice(0, ROWS), slice(0, 256))

from contextlib import ExitStack

import concourse.mybir as mybir
from concourse.masks import make_identity

T, R, F = 1536, 1024, 2048
FLOPS = 2 * T * R * F

F32 = mybir.dt.float32
BF16 = mybir.dt.bfloat16
I32 = mybir.dt.int32
U32 = mybir.dt.uint32
U8 = mybir.dt.uint8
FP8X4 = mybir.dt.float8_e4m3fn_x4
FP4X4 = mybir.dt.float4_e2m1fn_x4
ACT = mybir.ActivationFunctionType
ALU = mybir.AluOpType

P = 128
BANK = 512
PASSES = R // 512
ROWS = 4
TBLOCKS = T // 512
FGROUPS = F // 512
GROUPS = TBLOCKS * FGROUPS
STEPS = 2 * GROUPS
STEPS_PER_BLOCK = 2 * FGROUPS


def tile_weighted_kl_nmf_ratio_g4_kernel(
    tc, h, w_words, w_scales, background, v, weight, out_0, out_1, out_2
):
    nc = tc.nc
    with ExitStack() as ctx:
        keep = ctx.enter_context(tc.tile_pool(name="keep", bufs=1))
        work = ctx.enter_context(tc.tile_pool(name="work", bufs=2))
        psum = ctx.enter_context(tc.psum_pool(name="psum", bufs=1))
        ctx.enter_context(tc.manual_schedule())

        ident = keep.tile([P, P], F32, name="ident")
        bc_rows = keep.tile([P, P], BF16, name="bc_rows")
        rows_rsqrt = keep.tile([P, P], F32, name="rows_rsqrt")
        rows32 = keep.tile([P, 2, P], F32, name="rows32")
        bc = keep.tile([P, 2 * P], F32, name="bc")
        w_plane = keep.tile([P, PASSES, F], U8, name="w_plane", align_bytes=64)

        h_raw, h_words, h_bank, h_turned, h_codes, h_plane = {}, {}, {}, {}, {}, {}
        w_codes, v_raw = {}, {}
        mx_bank, ratio, r_bank, y, y_words, y_bank, y_turned, y_codes, y_plane = (
            {}, {}, {}, {}, {}, {}, {}, {}, {})

        def bank(tag):
            depth = {"mx": 2, "r": 3, "w": 1, "h": 2}[tag]
            return psum.tile([P, BANK], F32, name="bank_" + tag, tag=tag, bufs=depth)

        def load_h(tb, jj, passes):
            width = 512 * len(passes)
            t = work.tile([P, 2, width], BF16, name="h_raw%d" % width, bufs=4)
            r0, c0 = 512 * tb + 256 * jj, 512 * passes[0]
            src = h[r0 : r0 + 256, c0 : c0 + width]
            nc.sync.dma_start(out=t[:], in_=src.rearrange("(j p) k -> p j k", p=P))
            for n, ps in enumerate(passes):
                h_raw[tb, ps, jj] = t[:].bitcast(F32)[:, :, 256 * n : 256 * (n + 1)]

        def load_w(g0, g1):
            t = keep.tile([P, PASSES, 1024 * (g1 - g0)], U8, name="w_codes%d" % g0, align_bytes=64)
            src = w_words[:, :, 1024 * g0 : 1024 * g1].rearrange("s p b -> p s b")
            nc.sync.dma_start(out=t[:].bitcast(I32), in_=src.bitcast(I32))
            for g in range(g0, g1):
                w_codes[g] = t[:, :, 1024 * (g - g0) : 1024 * (g - g0 + 1)]

        def load_v(tb, g0, g1):
            t = keep.tile([P, ROWS, 512 * (g1 - g0)], BF16, name="v_raw%d_%d" % (tb, g0))
            src = v[512 * tb : 512 * (tb + 1), 512 * g0 : 512 * g1]
            nc.sync.dma_start(out=t[:], in_=src.rearrange("(j p) f -> p j f", p=P))
            for g in range(g0, g1):
                v_raw[FGROUPS * tb + g] = t[:, :, 512 * (g - g0) : 512 * (g - g0 + 1)]

        def sort_h(tb, ps, jj):
            t = work.tile([P, 2, 2, P], F32, name="h_words", bufs=4)
            src = h_raw[tb, ps, jj]
            nc.vector.tensor_copy(out=t[:], in_=src.rearrange("p j (q u) -> p j u q", u=2))
            h_words[tb, ps, jj] = t

        def turn_h(tb, ps, jj, tag, rows=(0, 1)):
            if rows[0] == 0:
                h_bank[tb, ps, jj] = bank(tag)
            b = h_bank[tb, ps, jj]
            for j2 in rows:
                for u in range(2):
                    if (tb, ps, jj) in h_words:
                        src = h_words[tb, ps, jj][:, j2, u, :]
                    else:
                        src = h_raw[tb, ps, jj][:, j2, u::2]
                    col = (2 * j2 + u) * P
                    nc.tensor.transpose(b[:, col : col + P], src, ident[:])

        def interleave(eng, dst, jj, b):
            out = dst[:].bitcast(F32)[:, 512 * jj : 512 * (jj + 1)].rearrange("p (j m u) -> p j m u", j=2, u=2)
            src = b[:].rearrange("p (j u m) -> p j m u", j=2, u=2)
            if eng == "scalar":
                nc.scalar.copy(out=out, in_=src)
            else:
                nc.vector.tensor_copy(out=out, in_=src)

        def drain_h(tb, ps, jj, eng):
            if jj == 0:
                h_turned[tb, ps] = work.tile([P, 2048], BF16, name="h_turned", bufs=2, align_bytes=64)
            interleave(eng, h_turned[tb, ps], jj, h_bank[tb, ps, jj])

        def quant_h(tb, ps, m0=0, m1=512):
            if m0 == 0:
                h_codes[tb, ps] = work.tile([P, 512], U32, name="h_codes", bufs=4, align_bytes=64)
                h_plane[tb, ps] = work.tile([P, 512], U8, name="h_plane", bufs=4, align_bytes=64)
            nc.vector.quantize_mx(out=h_codes[tb, ps][:, m0:m1].bitcast(FP8X4), scales=h_plane[tb, ps][:, m0:m1],
                                  in_=h_turned[tb, ps][:, 4 * m0 : 4 * m1])

        def multiply(k, order):
            tb, g, half = k // STEPS_PER_BLOCK, (k // 2) % FGROUPS, k % 2
            for b in range(2):
                mx_bank[k, b] = bank("mx")
            for b, ps in order:
                col = 256 * half + P * b
                nc.tensor.matmul_mx(
                    out=mx_bank[k, b][:],
                    lhsT=w_codes[g][:, ps, 2 * col : 2 * (col + P)].bitcast(FP4X4),
                    lhsT_scale=w_plane[:, ps, 512 * g + col : 512 * g + col + P],
                    rhs=h_codes[tb, ps][:].bitcast(FP8X4),
                    rhs_scale=h_plane[tb, ps][:],
                    start=(ps == 0),
                    stop=(ps == PASSES - 1),
                )

        def invert(k):
            fb0 = 2 * (k % STEPS_PER_BLOCK)
            root = work.tile([P, 2, BANK], F32, name="root", bufs=2)
            ratio[k] = work.tile([P, 2, BANK], F32, name="ratio", bufs=3)
            for b in range(2):
                nc.scalar.activation(out=root[:, b, :], in_=mx_bank[k, b][:], func=ACT.Abs_reciprocal_sqrt,
                                     bias=bc[:, fb0 + b : fb0 + b + 1])
            for b in range(2):
                nc.scalar.activation(out=ratio[k][:, b, :], in_=root[:, b, :], func=ACT.Square,
                                     scale=bc[:, P + 16 + fb0 + b : P + 16 + fb0 + b + 1])

        def turn_ratio(k):
            for jj in range(2):
                bk = bank("r")
                for j2 in range(2):
                    for b in range(2):
                        j = 2 * jj + j2
                        col = (2 * j2 + b) * P
                        nc.tensor.transpose(bk[:, col : col + P], ratio[k][:, b, P * j : P * (j + 1)], ident[:])
                r_bank[k, jj] = bk

        def apply_v(k, jj):
            grp, half = divmod(k, 2)
            if half == 0 and jj == 0:
                y[grp] = work.tile([P, ROWS, 512], F32, name="y", bufs=4)
            rows, cols = slice(2 * jj, 2 * jj + 2), slice(256 * half, 256 * (half + 1))
            nc.vector.tensor_tensor(
                out=y[grp][:, rows, cols],
                in0=r_bank[k, jj][:].rearrange("p (j f) -> p j f", j=2),
                in1=v_raw[grp][:, rows, cols],
                op=ALU.mult)

        def store_y(grp, rows, cols):
            tb, g = divmod(grp, FGROUPS)
            dst = out_0[512 * tb : 512 * (tb + 1), 512 * g : 512 * (g + 1)].rearrange("(j p) f -> p j f", p=P)
            nc.sync.dma_start(out=dst[:, rows, cols], in_=y[grp][:, rows, cols])

        def round_y(unit):
            grp, jj = divmod(unit, 2)
            t = work.tile([P, 2, 2 * P, 2], BF16, name="y_words", bufs=3)
            src = y[grp][:, 2 * jj : 2 * jj + 2, :].rearrange("p j (q u e) -> p u (j q) e", u=2, e=2)
            if unit < STEPS - 2:
                nc.gpsimd.tensor_scalar(out=t[:], in0=src, scalar1=1.0, scalar2=0.0, op0=ALU.mult, op1=ALU.add)
            else:
                nc.vector.tensor_copy(out=t[:], in_=src)
            y_words[unit] = t

        def turn_y(unit):
            b = bank("h" if unit >= STEPS - 4 and unit % 2 == 1 else "w")
            words = y_words[unit][:].rearrange("p u q e -> p (u q e)").bitcast(F32)
            for j2 in range(2):
                for u in range(2):
                    src0 = (2 * u + j2) * P
                    col = (2 * j2 + u) * P
                    nc.tensor.transpose(b[:, col : col + P], words[:, src0 : src0 + P], ident[:])
            y_bank[unit] = b

        def drain_y(unit, eng):
            grp, jj = divmod(unit, 2)
            if jj == 0:
                y_turned[grp] = work.tile([P, 2048], BF16, name="y_turned", bufs=2, align_bytes=64)
            interleave(eng, y_turned[grp], jj, y_bank[unit])

        def quant_y(grp, m0, m1):
            tb, g = divmod(grp, FGROUPS)
            if m0 == 0:
                if g == 0:
                    y_plane[tb] = work.tile([P, 512], U8, name="y_plane", bufs=2, align_bytes=64)
                y_codes[grp] = work.tile([P, 512], U32, name="y_codes", bufs=3, align_bytes=64)
            nc.vector.quantize_mx(out=y_codes[grp][:, m0:m1].bitcast(FP8X4), scales=y_plane[tb][4 * g :, m0:m1],
                                  in_=y_turned[grp][:, 4 * m0 : 4 * m1])
            dst = out_1[g, :, 512 * tb + m0 : 512 * tb + m1, :].rearrange("p m t -> p (m t)")
            nc.sync.dma_start(out=dst.bitcast(I32), in_=y_codes[grp][:, m0:m1].bitcast(I32))
            if g == FGROUPS - 1 and m1 == 512:
                for q in range(4):
                    dst = out_2[:, 4 * q : 4 * q + 4, 512 * tb : 512 * (tb + 1)]
                    queue = nc.scalar if (grp == GROUPS - 1 and q % 2 == 1) else nc.sync
                    queue.dma_start(out=dst.bitcast(I32), in_=y_plane[tb][32 * q : 32 * q + 16, :].bitcast(I32))

        nc.vector.memset(bc_rows[:], 0.0)
        nc.vector.memset(w_plane[:].bitcast(I32), 0)
        make_identity(nc, ident[:])
        nc.scalar.dma_start(out=bc_rows[0:16, :], in_=background.rearrange("(c p) -> c p", p=P))
        nc.scalar.dma_start(out=bc_rows[16:32, :], in_=weight.rearrange("(c p) -> c p", p=P))
        for ps in range(PASSES):
            for jj in range(2):
                load_h(0, jj, (ps,))
        for q in range(4):
            src = w_scales[:, 4 * q : 4 * q + 4, :].rearrange("s r n -> r s n")
            nc.sync.dma_start(out=w_plane[32 * q : 32 * q + 4].bitcast(I32), in_=src.bitcast(I32))
        load_w(0, 1)
        load_h(1, 0, (0, 1))
        load_v(0, 0, 1)
        load_h(1, 1, (0, 1))
        load_w(1, FGROUPS)
        load_v(0, 1, FGROUPS)
        load_h(2, 0, (0, 1))
        load_h(2, 1, (0, 1))
        load_v(1, 0, FGROUPS)

        nc.scalar.activation(out=rows_rsqrt[:], in_=bc_rows[:], func=ACT.Abs_reciprocal_sqrt, bias=2.0 ** -86)
        sort_h(0, 0, 0)
        sort_h(0, 0, 1)
        turn_h(0, 0, 0, "h")
        turn_h(0, 0, 1, "h")
        sort_h(0, 1, 0)
        sort_h(0, 1, 1)
        turn_h(0, 1, 0, "r")
        turn_h(0, 1, 1, "r")
        drain_h(0, 0, 0, "scalar")
        drain_h(0, 0, 1, "vector")
        nc.vector.tensor_copy(out=rows32[:, 0, :], in_=bc_rows[:])
        nc.vector.tensor_tensor(out=rows32[:, 1, :], in0=bc_rows[:], in1=rows_rsqrt[:], op=ALU.mult)
        bc_bank = bank("w")
        for i in range(2):
            nc.tensor.transpose(bc_bank[:, P * i : P * (i + 1)], rows32[:, i, :], ident[:])
        drain_h(0, 1, 0, "scalar")
        quant_h(0, 0)
        drain_h(0, 1, 1, "scalar")
        nc.scalar.copy(out=bc[:], in_=bc_bank[:, 0 : 2 * P])
        quant_h(0, 1, 0, 256)
        quant_h(0, 1, 256, 512)

        h_turns, h_drains, h_quants = {}, {}, {4: (1, 0), 6: (1, 1), 10: (2, 0), 14: (2, 1)}
        for c in range(4):
            ps, jj = divmod(c, 2)
            h_turns[c] = (1, ps, jj, "h", (0, 1))
            h_drains[c + 1] = (1, ps, jj)
            h_turns[5 + 2 * c] = (2, ps, jj, "h", (0,))
            h_turns[6 + 2 * c] = (2, ps, jj, "h", (1,))
            h_drains[7 + 2 * c] = (2, ps, jj)
        for k in range(STEPS + 5):
            if k == 6:
                load_v(2, 0, FGROUPS)
            if k < STEPS:
                multiply(k, [(0, 0), (1, 0), (0, 1), (1, 1)] if k == 0 else [(0, 0), (0, 1), (1, 0), (1, 1)])
                invert(k)
            if 0 <= k - 3 < STEPS:
                round_y(k - 3)
            if k in h_drains:
                drain_h(*h_drains[k], "vector")
            if 6 <= k < STEPS + 4 and k % 2 == 0:
                quant_y((k - 6) // 2, 0, 512)
            if k in h_quants:
                quant_h(*h_quants[k])
            if 0 <= k - 4 < STEPS:
                turn_y(k - 4)
                drain_y(k - 4, "scalar" if k >= STEPS else "vector")
            if k >= STEPS + 3:
                quant_y(GROUPS - 1, 256 * (k - STEPS - 3), 256 * (k - STEPS - 2))
            if k in h_turns:
                turn_h(*h_turns[k])
            if 0 <= k - 1 < STEPS:
                turn_ratio(k - 1)
                for jj in range(2):
                    apply_v(k - 1, jj)
                    if k == STEPS:
                        store_y(GROUPS - 1, slice(2 * jj, 2 * jj + 2), slice(256, 512))
                if k % 2 == 0 and k < STEPS:
                    store_y((k - 1) // 2, slice(0, ROWS), slice(0, 512))
                if k == STEPS - 1:
                    store_y(GROUPS - 1, slice(0, ROWS), slice(0, 256))
